import numpy as np
import ml_dtypes


def mxq(x, axis, fmt="e4m3"):
    dtype, down = {"e4m3": (ml_dtypes.float8_e4m3fn, 7), "e5m2": (ml_dtypes.float8_e5m2, 14)}[fmt]
    v = np.moveaxis(np.asarray(x, np.float32).astype(ml_dtypes.bfloat16).astype(np.float64), axis, -1)
    blocks = v.reshape(v.shape[:-1] + (-1, 32))
    amax = np.abs(blocks).max(-1, keepdims=True)
    byte = np.maximum(np.where(amax > 0, np.frexp(amax)[1] - 1 + 127, 0) - down, 1)
    scale = np.exp2(byte - 127.0)
    codes = (blocks / scale).astype(np.float32).astype(dtype).astype(np.float64)
    return np.moveaxis((codes * scale).reshape(v.shape), -1, axis)


WIDE = False


def mx_kscale(k):
    if not WIDE:
        return np.ones(k)
    levels = np.array([10, -10, 5, -5, 0])
    if k % 512:
        return np.exp2(np.random.permutation(np.resize(levels, k // 32))).repeat(32)
    a = np.empty((k // 512, 16))
    for p in range(k // 512):
        a[p, :8] = np.random.permutation(np.resize(levels, 8))
        for g in range(8):
            far = levels[np.abs(levels - a[p, g]) >= 10]
            a[p, g + 8] = far[np.random.randint(len(far))]
    return np.exp2(a.ravel()).repeat(32)


def f64(x):
    return np.asarray(x).astype(np.float64)


def striped(idx):
    return np.tile(idx.reshape(-1, 16).T, (8, 1)).astype(np.uint16)


def unstriped(offs):
    return offs[:16].T.reshape(-1).astype(np.int64)


def pack_weight(w):
    k, n = w.shape
    w = f64(np.asarray(w, np.float32).astype(ml_dtypes.bfloat16)).reshape(k // 32, 32, n)
    amax = np.abs(w).max(1)
    byte = np.clip(np.where(amax > 0, np.frexp(amax)[1] - 1 + 127 - 7, 1), 1, 254)
    scaled = (w * np.exp2(127.0 - byte)[:, None, :]).reshape(k, n).astype(np.float32)
    words = np.ascontiguousarray(scaled.reshape(k // 512, 128, 4, n).transpose(0, 1, 3, 2)).astype(ml_dtypes.float8_e4m3fn).view(np.uint8)
    return words, np.ascontiguousarray(byte.astype(np.uint8).reshape(k // 512, 16, n))


def unpack_weight(words, scales):
    g, p, n, _ = words.shape
    vals = np.ascontiguousarray(words).view(ml_dtypes.float8_e4m3fn).astype(np.float64) * np.repeat(np.exp2(scales.astype(np.float64) - 127.0), 8, axis=1)[..., None]
    return vals.transpose(0, 1, 3, 2).reshape(g * 512, n)


def silu(v):
    return v / (1.0 + np.exp(-np.maximum(v, -700.0)))


K, T, E, C, N = 512, 4096, 32, 128, 256


def by_expert(wq, xq):
    return np.concatenate([wq[e].T @ xq[:, e * C:(e + 1) * C] for e in range(E)], axis=1)


def setup_inputs():
    n = np.random.standard_normal
    s = mx_kscale(K)[:, None]
    packed = [pack_weight(m) for m in n((E, K, N)) / np.sqrt(K) / s[None]]
    return {
        "xT": (n((K, T)) * s).astype(np.float32),
        "w_words": np.stack([m[0] for m in packed]),
        "w_scales": np.stack([m[1] for m in packed]),
        "b": (0.3 * n((N, E))).astype(np.float32),
        "gate": np.tile(np.random.uniform(0.2, 1.0, E * C), (N, 1)).astype(np.float32),
        "offs": striped(np.random.permutation(T)[:E * C]),
    }


def reference(xT, w_words, w_scales, b, gate, offs):
    idx = unstriped(offs)
    xq = mxq(f64(xT)[:, idx], 0, "e4m3")
    w = np.stack([unpack_weight(w_words[e], w_scales[e]) for e in range(E)])
    y = by_expert(w, xq)
    y = silu(y + np.repeat(f64(b), C, axis=1))
    out = np.zeros((N, T))
    out[:, idx] = f64(gate) * y
    return out

@@ -1,0 +1,161 @@
+from contextlib import ExitStack
+
+import concourse.mybir as mybir
+
+K, T, E, C, N = 512, 4096, 32, 128, 256
+P = 128
+H = N // P
+FLOPS = 2 * K * N * E * C
+
+F32 = mybir.dt.float32
+BF16 = mybir.dt.bfloat16
+U32 = mybir.dt.uint32
+I32 = mybir.dt.int32
+U16 = mybir.dt.uint16
+U8 = mybir.dt.uint8
+FP8X4 = mybir.dt.float8_e4m3fn_x4
+SILU = mybir.ActivationFunctionType.Silu
+MULT = mybir.AluOpType.mult
+
+LOAD = 1024
+HALF = LOAD // 2
+EARLY = 2048
+LATE = (512, 512, 1024, 1024, 1024)
+SCATTER = 2048
+BANK = 512
+
+
+def tile_routed_moe_kernel(tc, xT, w_words, w_scales, b, gate, offs, out):
+    nc = tc.nc
+    with ExitStack() as ctx:
+        lists = ctx.enter_context(tc.tile_pool(name="lists", bufs=1))
+        keep = ctx.enter_context(tc.tile_pool(name="keep", bufs=1))
+        stage = ctx.enter_context(tc.tile_pool(name="stage", bufs=8))
+        psum = ctx.enter_context(tc.psum_pool(name="psum", bufs=8))
+
+        offsets = lists.tile([P, E * C // 16], U16, name="offsets")
+        nc.sync.dma_start(offsets[:], offs)
+
+        warm = keep.tile([P, 8], F32, name="warm")
+        nc.vector.memset(warm[:], 0.0)
+        nc.scalar.activation(out=warm[:, 0:1], in_=warm[:, 1:2], func=SILU)
+
+        w_sc = keep.tile([P, E * N], U8, name="w_sc", align_bytes=64)
+        nc.vector.memset(w_sc[:].bitcast(I32), 0)
+        w_sb = keep.tile([P, E * N], U32, name="w_sb", align_bytes=64)
+        bias = keep.tile([P, H, E], F32, name="bias")
+
+        pairs = [keep.tile([P, T, 2], BF16, name=f"pair{u}", align_bytes=64) for u in range(2)]
+        grouped = keep.tile([P, E * C, 4], BF16, name="grouped", align_bytes=64)
+        codes = keep.tile([P, E * C], U32, name="codes", align_bytes=64)
+        scales = keep.tile([P, E * C], U8, name="scales", align_bytes=64)
+        windows = [keep.tile([P, T], F32, name=f"window{h}", align_bytes=64) for h in range(H)]
+
+        planes = xT.rearrange("(p u j) n -> u p j n", u=2, j=2)
+        words = [pair[:].rearrange("p n j -> p (n j)").bitcast(U32) for pair in pairs]
+        slots = grouped[:].rearrange("p n t -> p (n t)").bitcast(U32).rearrange("p (n u) -> p n u", u=2)
+
+        def cast(u, c, half, raw, on_vector):
+            lo = c * LOAD + half * HALF
+            dst = pairs[u][:, lo:lo + HALF, :]
+            src = raw[:, :, half * HALF:(half + 1) * HALF].rearrange("p j n -> p n j")
+            if on_vector:
+                nc.vector.tensor_copy(dst, src)
+            else:
+                nc.scalar.copy(dst, src)
+
+        def gather(u, lo, hi):
+            nc.vector.tensor_copy(slots[:, lo:hi, u], words[u].indirect(offsets[:, lo // 16:hi // 16]))
+
+        chunks = T // LOAD
+        for u in range(2):
+            for c in range(chunks):
+                raw = stage.tile([P, 2, LOAD], F32, name="st", tag="st", align_bytes=64)
+                nc.sync.dma_start(raw[:], planes[u, :, :, c * LOAD:(c + 1) * LOAD])
+                for half in range(2):
+                    cast(u, c, half, raw, (u == 0 and half == 0) or (u == 1 and c == chunks - 1 and half == 1))
+            if u == 0:
+                for lo in range(0, E * C, EARLY):
+                    gather(0, lo, lo + EARLY)
+
+        sc_view = w_scales.rearrange("e a q n -> (a q) e n")
+        for q in range(4):
+            nc.sync.dma_start(
+                w_sc[32 * q:32 * q + 4, :].bitcast(I32).rearrange("p (e n) -> p e n", e=E),
+                sc_view[4 * q:4 * q + 4].bitcast(I32),
+            )
+        w_view = w_words.rearrange("e a p n r -> p (e a) (n r)")
+
+        def load_w(e0, e1):
+            nc.sync.dma_start(
+                w_sb[:, e0 * N:e1 * N].bitcast(I32).rearrange("p (e n) -> p e n", n=N),
+                w_view[:, e0:e1].bitcast(I32),
+            )
+
+        gates = {}
+
+        def load_gate(h, s):
+            g = stage.tile([P, SCATTER], F32, name="st", tag="st", align_bytes=64)
+            nc.sync.dma_start(g[:], gate[h * P:(h + 1) * P, s * SCATTER:(s + 1) * SCATTER])
+            gates[h, s] = g
+
+        load_w(0, 8)
+        nc.sync.dma_start(bias[:], b.rearrange("(h p) e -> p h e", p=P))
+        load_w(8, 16)
+        load_gate(0, 0)
+        load_gate(1, 0)
+        load_w(16, 24)
+        load_w(24, 32)
+        load_gate(0, 1)
+        load_gate(1, 1)
+
+        ys = {}
+        lo = 0
+        for size in LATE:
+            hi = lo + size
+            gather(1, lo, hi)
+            nc.vector.quantize_mx(
+                out=codes[:, lo:hi].bitcast(FP8X4),
+                scales=scales[:, lo:hi],
+                in_=grouped[:, lo:hi, :].rearrange("p n t -> p (n t)"),
+            )
+            for base in range(lo, hi, BANK):
+                s, at = divmod(base, SCATTER)
+                for h in range(H):
+                    if (h, s) not in ys:
+                        ys[h, s] = stage.tile([P, SCATTER], F32, name="st", tag="st", align_bytes=64)
+                    acc = psum.tile([P, BANK], F32, name="acc")
+                    for i in range(BANK // C):
+                        e = base // C + i
+                        w_cols = slice(e * N + h * P, e * N + (h + 1) * P)
+                        x_cols = slice(e * C, (e + 1) * C)
+                        nc.tensor.matmul_mx(
+                            out=acc[:, i * C:(i + 1) * C],
+                            lhsT=w_sb[:, w_cols].bitcast(FP8X4),
+                            lhsT_scale=w_sc[:, w_cols],
+                            rhs=codes[:, x_cols].bitcast(FP8X4),
+                            rhs_scale=scales[:, x_cols],
+                            start=True,
+                            stop=True,
+                        )
+                    for i in range(BANK // C):
+                        e = base // C + i
+                        nc.scalar.activation(
+                            out=ys[h, s][:, at + i * C:at + (i + 1) * C],
+                            in_=acc[:, i * C:(i + 1) * C],
+                            func=SILU,
+                            bias=bias[:, h, e:e + 1],
+                        )
+            lo = hi
+
+        per = SCATTER // 16
+        for s in range(E * C // SCATTER):
+            for h in range(H):
+                nc.vector.tensor_tensor(
+                    windows[h][:].indirect(offsets[:, s * per:(s + 1) * per]),
+                    ys[h, s][:],
+                    gates[h, s][:],
+                    MULT,
+                )
+        for h in range(H):
+            nc.sync.dma_start(out[h * P:(h + 1) * P, :], windows[h][:])

@@ -19,9 +19,9 @@ MULT = mybir.AluOpType.mult
 
 LOAD = 1024
 HALF = LOAD // 2
-EARLY = 2048
-LATE = (512, 512, 1024, 1024, 1024)
-SCATTER = 2048
+CHUNKS = ((0, 512), (512, 1024), (1024, 2048), (2048, 3072), (3072, 4096))
+EARLY = ((512, 2048), (2048, 4096))
+GATE = 2048
 BANK = 512
 
 
@@ -30,7 +30,9 @@ def tile_routed_moe_kernel(tc, xT, w_words, w_scales, b, gate, offs, out):
     with ExitStack() as ctx:
         lists = ctx.enter_context(tc.tile_pool(name="lists", bufs=1))
         keep = ctx.enter_context(tc.tile_pool(name="keep", bufs=1))
-        stage = ctx.enter_context(tc.tile_pool(name="stage", bufs=8))
+        stage = ctx.enter_context(tc.tile_pool(name="stage", bufs=9))
+        columns = ctx.enter_context(tc.tile_pool(name="columns", bufs=2))
+        results = ctx.enter_context(tc.tile_pool(name="results", bufs=6))
         psum = ctx.enter_context(tc.psum_pool(name="psum", bufs=8))
 
         offsets = lists.tile([P, E * C // 16], U16, name="offsets")
@@ -45,15 +47,13 @@ def tile_routed_moe_kernel(tc, xT, w_words, w_scales, b, gate, offs, out):
         w_sb = keep.tile([P, E * N], U32, name="w_sb", align_bytes=64)
         bias = keep.tile([P, H, E], F32, name="bias")
 
-        pairs = [keep.tile([P, T, 2], BF16, name=f"pair{u}", align_bytes=64) for u in range(2)]
-        grouped = keep.tile([P, E * C, 4], BF16, name="grouped", align_bytes=64)
+        pairs = [columns.tile([P, T, 2], BF16, name=f"pair{u}", tag="columns", align_bytes=64) for u in range(2)]
+        picked = keep.tile([P, 2, E * C], U32, name="picked", align_bytes=64)
         codes = keep.tile([P, E * C], U32, name="codes", align_bytes=64)
         scales = keep.tile([P, E * C], U8, name="scales", align_bytes=64)
-        windows = [keep.tile([P, T], F32, name=f"window{h}", align_bytes=64) for h in range(H)]
 
         planes = xT.rearrange("(p u j) n -> u p j n", u=2, j=2)
         words = [pair[:].rearrange("p n j -> p (n j)").bitcast(U32) for pair in pairs]
-        slots = grouped[:].rearrange("p n t -> p (n t)").bitcast(U32).rearrange("p (n u) -> p n u", u=2)
 
         def cast(u, c, half, raw, on_vector):
             lo = c * LOAD + half * HALF
@@ -64,9 +64,16 @@ def tile_routed_moe_kernel(tc, xT, w_words, w_scales, b, gate, offs, out):
             else:
                 nc.scalar.copy(dst, src)
 
-        def gather(u, lo, hi):
-            nc.vector.tensor_copy(slots[:, lo:hi, u], words[u].indirect(offsets[:, lo // 16:hi // 16]))
+        def gather(u, lo, hi, dst):
+            nc.vector.tensor_copy(dst, words[u].indirect(offsets[:, lo // 16:hi // 16]))
 
+        def grouped_tile(lo, hi):
+            return stage.tile([P, hi - lo, 4], BF16, name="st", tag="st", align_bytes=64)
+
+        def grouped_words(grouped):
+            return grouped[:].rearrange("p n t -> p (n t)").bitcast(U32).rearrange("p (n u) -> p n u", u=2)
+
+        first = None
         chunks = T // LOAD
         for u in range(2):
             for c in range(chunks):
@@ -75,8 +82,10 @@ def tile_routed_moe_kernel(tc, xT, w_words, w_scales, b, gate, offs, out):
                 for half in range(2):
                     cast(u, c, half, raw, (u == 0 and half == 0) or (u == 1 and c == chunks - 1 and half == 1))
             if u == 0:
-                for lo in range(0, E * C, EARLY):
-                    gather(0, lo, lo + EARLY)
+                first = grouped_tile(*CHUNKS[0])
+                gather(0, *CHUNKS[0], grouped_words(first)[:, :, 0])
+                for lo, hi in EARLY:
+                    gather(0, lo, hi, picked[:, 0, lo:hi])
 
         sc_view = w_scales.rearrange("e a q n -> (a q) e n")
         for q in range(4):
@@ -95,8 +104,8 @@ def tile_routed_moe_kernel(tc, xT, w_words, w_scales, b, gate, offs, out):
         gates = {}
 
         def load_gate(h, s):
-            g = stage.tile([P, SCATTER], F32, name="st", tag="st", align_bytes=64)
-            nc.sync.dma_start(g[:], gate[h * P:(h + 1) * P, s * SCATTER:(s + 1) * SCATTER])
+            g = stage.tile([P, GATE], F32, name="st", tag="st", align_bytes=64)
+            nc.sync.dma_start(g[:], gate[h * P:(h + 1) * P, s * GATE:(s + 1) * GATE])
             gates[h, s] = g
 
         load_w(0, 8)
@@ -110,20 +119,27 @@ def tile_routed_moe_kernel(tc, xT, w_words, w_scales, b, gate, offs, out):
         load_gate(1, 1)
 
         ys = {}
-        lo = 0
-        for size in LATE:
-            hi = lo + size
-            gather(1, lo, hi)
+        for lo, hi in CHUNKS:
+            if lo == 0:
+                grouped = first
+                gather(1, lo, hi, grouped_words(grouped)[:, :, 1])
+            else:
+                gather(1, lo, hi, picked[:, 1, lo:hi])
+                grouped = grouped_tile(lo, hi)
+                nc.scalar.copy(
+                    grouped[:].rearrange("p n (u j) -> p n u j", u=2),
+                    picked[:, :, lo:hi].bitcast(BF16).rearrange("p u (n j) -> p n u j", j=2),
+                )
             nc.vector.quantize_mx(
                 out=codes[:, lo:hi].bitcast(FP8X4),
                 scales=scales[:, lo:hi],
-                in_=grouped[:, lo:hi, :].rearrange("p n t -> p (n t)"),
+                in_=grouped[:].rearrange("p n t -> p (n t)"),
             )
+            for h in range(H):
+                ys[h, lo] = results.tile([P, hi - lo], F32, name="y", align_bytes=64)
             for base in range(lo, hi, BANK):
-                s, at = divmod(base, SCATTER)
+                at = base - lo
                 for h in range(H):
-                    if (h, s) not in ys:
-                        ys[h, s] = stage.tile([P, SCATTER], F32, name="st", tag="st", align_bytes=64)
                     acc = psum.tile([P, BANK], F32, name="acc")
                     for i in range(BANK // C):
                         e = base // C + i
@@ -141,20 +157,20 @@ def tile_routed_moe_kernel(tc, xT, w_words, w_scales, b, gate, offs, out):
                     for i in range(BANK // C):
                         e = base // C + i
                         nc.scalar.activation(
-                            out=ys[h, s][:, at + i * C:at + (i + 1) * C],
+                            out=ys[h, lo][:, at + i * C:at + (i + 1) * C],
                             in_=acc[:, i * C:(i + 1) * C],
                             func=SILU,
                             bias=bias[:, h, e:e + 1],
                         )
-            lo = hi
 
-        per = SCATTER // 16
-        for s in range(E * C // SCATTER):
+        windows = [columns.tile([P, T], F32, name=f"window{h}", tag="columns", align_bytes=64) for h in range(H)]
+        for lo, hi in CHUNKS:
+            s, at = divmod(lo, GATE)
             for h in range(H):
                 nc.vector.tensor_tensor(
-                    windows[h][:].indirect(offsets[:, s * per:(s + 1) * per]),
-                    ys[h, s][:],
-                    gates[h, s][:],
+                    windows[h][:].indirect(offsets[:, lo // 16:hi // 16]),
+                    ys[h, lo][:],
+                    gates[h, s][:, at:at + hi - lo],
                     MULT,
                 )
         for h in range(H):

@@ -17,11 +17,12 @@ FP8X4 = mybir.dt.float8_e4m3fn_x4
 SILU = mybir.ActivationFunctionType.Silu
 MULT = mybir.AluOpType.mult
 
-LOAD = 1024
-HALF = LOAD // 2
-CHUNKS = ((0, 512), (512, 1024), (1024, 2048), (2048, 3072), (3072, 4096))
-EARLY = ((512, 2048), (2048, 4096))
+LOADS = ((0, 1024), (1024, 2048), (2048, 3072), (3072, 3584), (3584, 4096))
+STEP = 512
+PICKS = ((0, 1024), (1024, 2048), (2048, 4096))
+CHUNK = 1024
 GATE = 2048
+EARLY = ((0, 2048), (2048, 4096))
 BANK = 512
 
 
@@ -32,7 +33,7 @@ def tile_routed_moe_kernel(tc, xT, w_words, w_scales, b, gate, offs, out):
         keep = ctx.enter_context(tc.tile_pool(name="keep", bufs=1))
         stage = ctx.enter_context(tc.tile_pool(name="stage", bufs=9))
         columns = ctx.enter_context(tc.tile_pool(name="columns", bufs=2))
-        results = ctx.enter_context(tc.tile_pool(name="results", bufs=6))
+        results = ctx.enter_context(tc.tile_pool(name="results", bufs=1))
         psum = ctx.enter_context(tc.psum_pool(name="psum", bufs=8))
 
         offsets = lists.tile([P, E * C // 16], U16, name="offsets")
@@ -55,37 +56,37 @@ def tile_routed_moe_kernel(tc, xT, w_words, w_scales, b, gate, offs, out):
         planes = xT.rearrange("(p u j) n -> u p j n", u=2, j=2)
         words = [pair[:].rearrange("p n j -> p (n j)").bitcast(U32) for pair in pairs]
 
-        def cast(u, c, half, raw, on_vector):
-            lo = c * LOAD + half * HALF
-            dst = pairs[u][:, lo:lo + HALF, :]
-            src = raw[:, :, half * HALF:(half + 1) * HALF].rearrange("p j n -> p n j")
-            if on_vector:
-                nc.vector.tensor_copy(dst, src)
-            else:
-                nc.scalar.copy(dst, src)
+        def cast(u, lo, hi, raw, base, engine):
+            if hi > lo:
+                engine(pairs[u][:, lo:hi, :], raw[:, :, lo - base:hi - base].rearrange("p j n -> p n j"))
 
         def gather(u, lo, hi, dst):
             nc.vector.tensor_copy(dst, words[u].indirect(offsets[:, lo // 16:hi // 16]))
 
-        def grouped_tile(lo, hi):
-            return stage.tile([P, hi - lo, 4], BF16, name="st", tag="st", align_bytes=64)
-
-        def grouped_words(grouped):
-            return grouped[:].rearrange("p n t -> p (n t)").bitcast(U32).rearrange("p (n u) -> p n u", u=2)
-
-        first = None
-        chunks = T // LOAD
+        grouped = {}
         for u in range(2):
-            for c in range(chunks):
-                raw = stage.tile([P, 2, LOAD], F32, name="st", tag="st", align_bytes=64)
-                nc.sync.dma_start(raw[:], planes[u, :, :, c * LOAD:(c + 1) * LOAD])
-                for half in range(2):
-                    cast(u, c, half, raw, (u == 0 and half == 0) or (u == 1 and c == chunks - 1 and half == 1))
+            for lo, hi in LOADS:
+                raw = stage.tile([P, 2, hi - lo], F32, name="st", tag="st", align_bytes=64)
+                nc.sync.dma_start(raw[:], planes[u, :, :, lo:hi])
+                if u == 1 and hi <= 3072:
+                    for at in range(lo, hi, STEP):
+                        cast(u, at, at + STEP, raw, lo, nc.scalar.copy)
+                elif u == 1 and hi <= 3584:
+                    cast(u, lo, hi, raw, lo, nc.vector.tensor_copy)
+                else:
+                    mid = (lo + hi) // 2
+                    cast(u, lo, mid, raw, lo, nc.vector.tensor_copy)
+                    cast(u, mid, hi, raw, lo, nc.scalar.copy)
             if u == 0:
-                first = grouped_tile(*CHUNKS[0])
-                gather(0, *CHUNKS[0], grouped_words(first)[:, :, 0])
                 for lo, hi in EARLY:
                     gather(0, lo, hi, picked[:, 0, lo:hi])
+
+        gates = {}
+
+        def load_gate(h, s):
+            g = stage.tile([P, GATE], F32, name="st", tag="st", align_bytes=64)
+            nc.sync.dma_start(g[:], gate[h * P:(h + 1) * P, s * GATE:(s + 1) * GATE])
+            gates[h, s] = g
 
         sc_view = w_scales.rearrange("e a q n -> (a q) e n")
         for q in range(4):
@@ -101,76 +102,89 @@ def tile_routed_moe_kernel(tc, xT, w_words, w_scales, b, gate, offs, out):
                 w_view[:, e0:e1].bitcast(I32),
             )
 
-        gates = {}
-
-        def load_gate(h, s):
-            g = stage.tile([P, GATE], F32, name="st", tag="st", align_bytes=64)
-            nc.sync.dma_start(g[:], gate[h * P:(h + 1) * P, s * GATE:(s + 1) * GATE])
-            gates[h, s] = g
-
         load_w(0, 8)
         nc.sync.dma_start(bias[:], b.rearrange("(h p) e -> p h e", p=P))
         load_w(8, 16)
-        load_gate(0, 0)
-        load_gate(1, 0)
+        for h in range(H):
+            load_gate(h, 0)
         load_w(16, 24)
         load_w(24, 32)
-        load_gate(0, 1)
-        load_gate(1, 1)
+        for h in range(H):
+            load_gate(h, 1)
+
+        def interleave(c):
+            grouped[c] = stage.tile([P, CHUNK, 4], BF16, name="st", tag="st", align_bytes=64)
+            for at in range(0, CHUNK, STEP):
+                lo = c * CHUNK + at
+                src = picked[:, :, lo:lo + STEP]
+                dst = grouped[c][:, at:at + STEP, :]
+                if c < 2:
+                    nc.scalar.copy(
+                        dst.rearrange("p n (u j) -> p n u j", u=2),
+                        src.bitcast(BF16).rearrange("p u (n j) -> p n u j", j=2),
+                    )
+                else:
+                    nc.gpsimd.tensor_copy(
+                        dst.rearrange("p n t -> p (n t)").bitcast(U32).rearrange("p (n u) -> p n u", u=2),
+                        src.rearrange("p u n -> p n u"),
+                    )
+
+        def quantize(c):
+            cols = slice(c * CHUNK, (c + 1) * CHUNK)
+            nc.vector.quantize_mx(
+                out=codes[:, cols].bitcast(FP8X4),
+                scales=scales[:, cols],
+                in_=grouped[c][:].rearrange("p n t -> p (n t)"),
+            )
 
         ys = {}
-        for lo, hi in CHUNKS:
-            if lo == 0:
-                grouped = first
-                gather(1, lo, hi, grouped_words(grouped)[:, :, 1])
-            else:
-                gather(1, lo, hi, picked[:, 1, lo:hi])
-                grouped = grouped_tile(lo, hi)
-                nc.scalar.copy(
-                    grouped[:].rearrange("p n (u j) -> p n u j", u=2),
-                    picked[:, :, lo:hi].bitcast(BF16).rearrange("p u (n j) -> p n u j", j=2),
-                )
-            nc.vector.quantize_mx(
-                out=codes[:, lo:hi].bitcast(FP8X4),
-                scales=scales[:, lo:hi],
-                in_=grouped[:].rearrange("p n t -> p (n t)"),
-            )
+
+        def experts(s, h):
+            lo, hi = PICKS[s]
+            y = ys[s, h] = results.tile([P, hi - lo], F32, name=f"y{s}_{h}", align_bytes=64)
+            for at in range(0, hi - lo, BANK):
+                acc = psum.tile([P, BANK], F32, name="acc")
+                for i in range(BANK // C):
+                    e = (lo + at) // C + i
+                    w_cols = slice(e * N + h * P, e * N + (h + 1) * P)
+                    x_cols = slice(e * C, (e + 1) * C)
+                    nc.tensor.matmul_mx(
+                        out=acc[:, i * C:(i + 1) * C],
+                        lhsT=w_sb[:, w_cols].bitcast(FP8X4),
+                        lhsT_scale=w_sc[:, w_cols],
+                        rhs=codes[:, x_cols].bitcast(FP8X4),
+                        rhs_scale=scales[:, x_cols],
+                        start=True,
+                        stop=True,
+                    )
+                for i in range(BANK // C):
+                    e = (lo + at) // C + i
+                    nc.scalar.activation(
+                        out=y[:, at + i * C:at + (i + 1) * C],
+                        in_=acc[:, i * C:(i + 1) * C],
+                        func=SILU,
+                        bias=bias[:, h, e:e + 1],
+                    )
+
+        for c in range(T // CHUNK):
+            lo, hi = c * CHUNK, (c + 1) * CHUNK
+            gather(1, lo, hi, picked[:, 1, lo:hi])
+            interleave(c)
+        for c in range(T // CHUNK):
+            quantize(c)
+        for s in range(len(PICKS)):
             for h in range(H):
-                ys[h, lo] = results.tile([P, hi - lo], F32, name="y", align_bytes=64)
-            for base in range(lo, hi, BANK):
-                at = base - lo
-                for h in range(H):
-                    acc = psum.tile([P, BANK], F32, name="acc")
-                    for i in range(BANK // C):
-                        e = base // C + i
-                        w_cols = slice(e * N + h * P, e * N + (h + 1) * P)
-                        x_cols = slice(e * C, (e + 1) * C)
-                        nc.tensor.matmul_mx(
-                            out=acc[:, i * C:(i + 1) * C],
-                            lhsT=w_sb[:, w_cols].bitcast(FP8X4),
-                            lhsT_scale=w_sc[:, w_cols],
-                            rhs=codes[:, x_cols].bitcast(FP8X4),
-                            rhs_scale=scales[:, x_cols],
-                            start=True,
-                            stop=True,
-                        )
-                    for i in range(BANK // C):
-                        e = base // C + i
-                        nc.scalar.activation(
-                            out=ys[h, lo][:, at + i * C:at + (i + 1) * C],
-                            in_=acc[:, i * C:(i + 1) * C],
-                            func=SILU,
-                            bias=bias[:, h, e:e + 1],
-                        )
+                experts(s, h)
 
         windows = [columns.tile([P, T], F32, name=f"window{h}", tag="columns", align_bytes=64) for h in range(H)]
-        for lo, hi in CHUNKS:
-            s, at = divmod(lo, GATE)
+        for s in range(len(PICKS)):
+            lo, hi = PICKS[s]
+            t, at = divmod(lo, GATE)
             for h in range(H):
                 nc.vector.tensor_tensor(
                     windows[h][:].indirect(offsets[:, lo // 16:hi // 16]),
-                    ys[h, lo][:],
-                    gates[h, s][:, at:at + hi - lo],
+                    ys[s, h][:],
+                    gates[h, t][:, at:at + hi - lo],
                     MULT,
                 )
         for h in range(H):

@@ -68,11 +68,9 @@ def tile_routed_moe_kernel(tc, xT, w_words, w_scales, b, gate, offs, out):
             for lo, hi in LOADS:
                 raw = stage.tile([P, 2, hi - lo], F32, name="st", tag="st", align_bytes=64)
                 nc.sync.dma_start(raw[:], planes[u, :, :, lo:hi])
-                if u == 1 and hi <= 3072:
+                if u == 1 and hi < T:
                     for at in range(lo, hi, STEP):
                         cast(u, at, at + STEP, raw, lo, nc.scalar.copy)
-                elif u == 1 and hi <= 3584:
-                    cast(u, lo, hi, raw, lo, nc.vector.tensor_copy)
                 else:
                     mid = (lo + hi) // 2
                     cast(u, lo, mid, raw, lo, nc.vector.tensor_copy)
@@ -116,18 +114,10 @@ def tile_routed_moe_kernel(tc, xT, w_words, w_scales, b, gate, offs, out):
             grouped[c] = stage.tile([P, CHUNK, 4], BF16, name="st", tag="st", align_bytes=64)
             for at in range(0, CHUNK, STEP):
                 lo = c * CHUNK + at
-                src = picked[:, :, lo:lo + STEP]
-                dst = grouped[c][:, at:at + STEP, :]
-                if c < 2:
-                    nc.scalar.copy(
-                        dst.rearrange("p n (u j) -> p n u j", u=2),
-                        src.bitcast(BF16).rearrange("p u (n j) -> p n u j", j=2),
-                    )
-                else:
-                    nc.gpsimd.tensor_copy(
-                        dst.rearrange("p n t -> p (n t)").bitcast(U32).rearrange("p (n u) -> p n u", u=2),
-                        src.rearrange("p u n -> p n u"),
-                    )
+                nc.scalar.copy(
+                    grouped[c][:, at:at + STEP, :].rearrange("p n t -> p (n t)").bitcast(F32).rearrange("p (n u) -> p n u", u=2),
+                    picked[:, :, lo:lo + STEP].bitcast(F32).rearrange("p u n -> p n u"),
+                )
 
         def quantize(c):
             cols = slice(c * CHUNK, (c + 1) * CHUNK)

from contextlib import ExitStack

import concourse.mybir as mybir

K, T, E, C, N = 512, 4096, 32, 128, 256
P = 128
H = N // P
FLOPS = 2 * K * N * E * C

F32 = mybir.dt.float32
BF16 = mybir.dt.bfloat16
U32 = mybir.dt.uint32
I32 = mybir.dt.int32
U16 = mybir.dt.uint16
U8 = mybir.dt.uint8
FP8X4 = mybir.dt.float8_e4m3fn_x4
SILU = mybir.ActivationFunctionType.Silu
MULT = mybir.AluOpType.mult

LOADS = ((0, 1024), (1024, 2048), (2048, 3072), (3072, 3584), (3584, 4096))
STEP = 512
PICKS = ((0, 1024), (1024, 2048), (2048, 4096))
CHUNK = 1024
GATE = 2048
EARLY = ((0, 2048), (2048, 4096))
BANK = 512


def tile_routed_moe_kernel(tc, xT, w_words, w_scales, b, gate, offs, out):
    nc = tc.nc
    with ExitStack() as ctx:
        lists = ctx.enter_context(tc.tile_pool(name="lists", bufs=1))
        keep = ctx.enter_context(tc.tile_pool(name="keep", bufs=1))
        stage = ctx.enter_context(tc.tile_pool(name="stage", bufs=9))
        columns = ctx.enter_context(tc.tile_pool(name="columns", bufs=2))
        results = ctx.enter_context(tc.tile_pool(name="results", bufs=1))
        psum = ctx.enter_context(tc.psum_pool(name="psum", bufs=8))

        offsets = lists.tile([P, E * C // 16], U16, name="offsets")
        nc.sync.dma_start(offsets[:], offs)

        warm = keep.tile([P, 8], F32, name="warm")
        nc.vector.memset(warm[:], 0.0)
        nc.scalar.activation(out=warm[:, 0:1], in_=warm[:, 1:2], func=SILU)

        w_sc = keep.tile([P, E * N], U8, name="w_sc", align_bytes=64)
        nc.vector.memset(w_sc[:].bitcast(I32), 0)
        w_sb = keep.tile([P, E * N], U32, name="w_sb", align_bytes=64)
        bias = keep.tile([P, H, E], F32, name="bias")

        pairs = [columns.tile([P, T, 2], BF16, name=f"pair{u}", tag="columns", align_bytes=64) for u in range(2)]
        picked = keep.tile([P, 2, E * C], U32, name="picked", align_bytes=64)
        codes = keep.tile([P, E * C], U32, name="codes", align_bytes=64)
        scales = keep.tile([P, E * C], U8, name="scales", align_bytes=64)

        planes = xT.rearrange("(p u j) n -> u p j n", u=2, j=2)
        words = [pair[:].rearrange("p n j -> p (n j)").bitcast(U32) for pair in pairs]

        def cast(u, lo, hi, raw, base, engine):
            if hi > lo:
                engine(pairs[u][:, lo:hi, :], raw[:, :, lo - base:hi - base].rearrange("p j n -> p n j"))

        def gather(u, lo, hi, dst):
            nc.vector.tensor_copy(dst, words[u].indirect(offsets[:, lo // 16:hi // 16]))

        grouped = {}
        for u in range(2):
            for lo, hi in LOADS:
                raw = stage.tile([P, 2, hi - lo], F32, name="st", tag="st", align_bytes=64)
                nc.sync.dma_start(raw[:], planes[u, :, :, lo:hi])
                if u == 1 and hi < T:
                    for at in range(lo, hi, STEP):
                        cast(u, at, at + STEP, raw, lo, nc.scalar.copy)
                else:
                    mid = (lo + hi) // 2
                    cast(u, lo, mid, raw, lo, nc.vector.tensor_copy)
                    cast(u, mid, hi, raw, lo, nc.scalar.copy)
            if u == 0:
                for lo, hi in EARLY:
                    gather(0, lo, hi, picked[:, 0, lo:hi])

        gates = {}

        def load_gate(h, s):
            g = stage.tile([P, GATE], F32, name="st", tag="st", align_bytes=64)
            nc.sync.dma_start(g[:], gate[h * P:(h + 1) * P, s * GATE:(s + 1) * GATE])
            gates[h, s] = g

        sc_view = w_scales.rearrange("e a q n -> (a q) e n")
        for q in range(4):
            nc.sync.dma_start(
                w_sc[32 * q:32 * q + 4, :].bitcast(I32).rearrange("p (e n) -> p e n", e=E),
                sc_view[4 * q:4 * q + 4].bitcast(I32),
            )
        w_view = w_words.rearrange("e a p n r -> p (e a) (n r)")

        def load_w(e0, e1):
            nc.sync.dma_start(
                w_sb[:, e0 * N:e1 * N].bitcast(I32).rearrange("p (e n) -> p e n", n=N),
                w_view[:, e0:e1].bitcast(I32),
            )

        load_w(0, 8)
        nc.sync.dma_start(bias[:], b.rearrange("(h p) e -> p h e", p=P))
        load_w(8, 16)
        for h in range(H):
            load_gate(h, 0)
        load_w(16, 24)
        load_w(24, 32)
        for h in range(H):
            load_gate(h, 1)

        def interleave(c):
            grouped[c] = stage.tile([P, CHUNK, 4], BF16, name="st", tag="st", align_bytes=64)
            for at in range(0, CHUNK, STEP):
                lo = c * CHUNK + at
                nc.scalar.copy(
                    grouped[c][:, at:at + STEP, :].rearrange("p n t -> p (n t)").bitcast(F32).rearrange("p (n u) -> p n u", u=2),
                    picked[:, :, lo:lo + STEP].bitcast(F32).rearrange("p u n -> p n u"),
                )

        def quantize(c):
            cols = slice(c * CHUNK, (c + 1) * CHUNK)
            nc.vector.quantize_mx(
                out=codes[:, cols].bitcast(FP8X4),
                scales=scales[:, cols],
                in_=grouped[c][:].rearrange("p n t -> p (n t)"),
            )

        ys = {}

        def experts(s, h):
            lo, hi = PICKS[s]
            y = ys[s, h] = results.tile([P, hi - lo], F32, name=f"y{s}_{h}", align_bytes=64)
            for at in range(0, hi - lo, BANK):
                acc = psum.tile([P, BANK], F32, name="acc")
                for i in range(BANK // C):
                    e = (lo + at) // C + i
                    w_cols = slice(e * N + h * P, e * N + (h + 1) * P)
                    x_cols = slice(e * C, (e + 1) * C)
                    nc.tensor.matmul_mx(
                        out=acc[:, i * C:(i + 1) * C],
                        lhsT=w_sb[:, w_cols].bitcast(FP8X4),
                        lhsT_scale=w_sc[:, w_cols],
                        rhs=codes[:, x_cols].bitcast(FP8X4),
                        rhs_scale=scales[:, x_cols],
                        start=True,
                        stop=True,
                    )
                for i in range(BANK // C):
                    e = (lo + at) // C + i
                    nc.scalar.activation(
                        out=y[:, at + i * C:at + (i + 1) * C],
                        in_=acc[:, i * C:(i + 1) * C],
                        func=SILU,
                        bias=bias[:, h, e:e + 1],
                    )

        for c in range(T // CHUNK):
            lo, hi = c * CHUNK, (c + 1) * CHUNK
            gather(1, lo, hi, picked[:, 1, lo:hi])
            interleave(c)
        for c in range(T // CHUNK):
            quantize(c)
        for s in range(len(PICKS)):
            for h in range(H):
                experts(s, h)

        windows = [columns.tile([P, T], F32, name=f"window{h}", tag="columns", align_bytes=64) for h in range(H)]
        for s in range(len(PICKS)):
            lo, hi = PICKS[s]
            t, at = divmod(lo, GATE)
            for h in range(H):
                nc.vector.tensor_tensor(
                    windows[h][:].indirect(offsets[:, lo // 16:hi // 16]),
                    ys[s, h][:],
                    gates[h, t][:, at:at + hi - lo],
                    MULT,
                )
        for h in range(H):
            nc.sync.dma_start(out[h * P:(h + 1) * P, :], windows[h][:])
